import numpy as np
import ml_dtypes


def mxq(x, axis, fmt="e4m3"):
    dtype, down = {"e4m3": (ml_dtypes.float8_e4m3fn, 7), "e5m2": (ml_dtypes.float8_e5m2, 14)}[fmt]
    v = np.moveaxis(np.asarray(x, np.float32).astype(ml_dtypes.bfloat16).astype(np.float64), axis, -1)
    blocks = v.reshape(v.shape[:-1] + (-1, 32))
    amax = np.abs(blocks).max(-1, keepdims=True)
    byte = np.maximum(np.where(amax > 0, np.frexp(amax)[1] - 1 + 127, 0) - down, 1)
    scale = np.exp2(byte - 127.0)
    codes = (blocks / scale).astype(np.float32).astype(dtype).astype(np.float64)
    return np.moveaxis((codes * scale).reshape(v.shape), -1, axis)


WIDE = False


def mx_kscale(k):
    if not WIDE:
        return np.ones(k)
    levels = np.array([30, -30])
    if k % 512:
        return np.exp2(np.random.permutation(np.resize(levels, k // 32))).repeat(32)
    a = np.empty((k // 512, 16))
    for p in range(k // 512):
        a[p, :8] = np.random.permutation(np.resize(levels, 8))
        for g in range(8):
            far = levels[np.abs(levels - a[p, g]) >= 10]
            a[p, g + 8] = far[np.random.randint(len(far))]
    return np.exp2(a.ravel()).repeat(32)


def f64(x):
    return np.asarray(x).astype(np.float64)


def striped(idx):
    return np.tile(np.asarray(idx).reshape(-1, 16).T, (8, 1)).astype(np.uint16)


def unstriped(offs):
    return offs[:16].T.reshape(-1).astype(np.int64)


E2M1 = np.array([0.0, 0.5, 1.0, 1.5, 2.0, 3.0, 4.0, 6.0, -0.0, -0.5, -1.0, -1.5, -2.0, -3.0, -4.0, -6.0])


def pack_weight(w, fmt):
    k, n = w.shape
    w = f64(np.asarray(w, np.float32).astype(ml_dtypes.bfloat16)).reshape(k // 32, 32, n)
    amax = np.abs(w).max(1)
    if fmt in ("e4m3", "e5m2"):
        byte = np.frexp(amax)[1] - 1 + 127 - (7 if fmt == "e4m3" else 14)
    else:
        mant, ex = np.frexp(amax / 6.0)
        byte = np.where(mant > 0.5, ex, ex - 1) + 127
    byte = np.clip(np.where(amax > 0, byte, 1), 1, 254)
    scaled = (w * np.exp2(127.0 - byte)[:, None, :]).reshape(k, n).astype(np.float32)
    by_word = np.ascontiguousarray(scaled.reshape(k // 512, 128, 4, n).transpose(0, 1, 3, 2))
    if fmt in ("e4m3", "e5m2"):
        words = by_word.astype(ml_dtypes.float8_e4m3fn if fmt == "e4m3" else ml_dtypes.float8_e5m2).view(np.uint8)
    else:
        c = by_word.astype(ml_dtypes.float4_e2m1fn).view(np.uint8) & 0xF
        words = (c[..., 0::2] | (c[..., 1::2] << 4)).reshape(k // 512, 128, 2 * n)
    return np.ascontiguousarray(words), np.ascontiguousarray(byte.astype(np.uint8).reshape(k // 512, 16, n))


def unpack_weight(words, scales, fmt):
    g, _, n = scales.shape
    words = np.ascontiguousarray(words).reshape(g, 128, n, -1)
    if fmt in ("e4m3", "e5m2"):
        vals = words.view(ml_dtypes.float8_e4m3fn if fmt == "e4m3" else ml_dtypes.float8_e5m2).astype(np.float64)
    else:
        nib = np.empty((g, 128, n, 4), np.uint8)
        nib[..., 0::2] = words & 0xF
        nib[..., 1::2] = words >> 4
        vals = E2M1[nib]
    vals = vals * np.repeat(np.exp2(scales.astype(np.float64) - 127.0), 8, axis=1)[..., None]
    return vals.transpose(0, 1, 3, 2).reshape(g * 512, n)


def sigmoid(v):
    return 1.0 / (1.0 + np.exp(-v))


K, T, J, R, F, Z, N = 512, 512, 256, 512, 512, 1024, 256


def setup_inputs():
    n = np.random.standard_normal
    idx = np.random.permutation(T)[:J]
    idx2 = np.random.permutation(T)[:J]
    idx3 = np.random.permutation(Z)[:J]
    fk = mx_kscale(K)
    fr = mx_kscale(R)
    ff = mx_kscale(F)
    wp = pack_weight(n((K, R)) * 1 / np.sqrt(K) * fk[:, None] * fr, "e5m2")
    w2p = pack_weight(n((F, R)) * 1 / np.sqrt(F) * ff[:, None] * fr, "e5m2")
    wbp = pack_weight(n((R, N)) * 1 / np.sqrt(R) / fr[:, None], "e4m3")
    return {
        "xf": (n((K, T))).astype(np.float32),
        "fk": (np.random.uniform(0.5, 2.0, (K, 1)) / fk[:, None]).astype(np.float32),
        "w_words": wp[0],
        "w_scales": wp[1],
        "xo": (n((F, Z))).astype(np.float32),
        "fl": (np.random.uniform(0.5, 2.0, (F, 1)) / ff[:, None]).astype(np.float32),
        "so": (n((F, J))).astype(np.float32),
        "w2_words": w2p[0],
        "w2_scales": w2p[1],
        "wb_words": wbp[0],
        "wb_scales": wbp[1],
        "rs": (1.0 * n((J, N))).astype(np.float32),
        "offs": striped(idx),
        "offs2": striped(idx2),
        "offs3": striped(idx3),
    }


def reference(xf, fk, w_words, w_scales, xo, fl, so, w2_words, w2_scales, wb_words, wb_scales, rs, offs, offs2, offs3):
    idx = unstriped(offs)
    idx2 = unstriped(offs2)
    idx3 = unstriped(offs3)
    wu = unpack_weight(w_words, w_scales, "e5m2")
    w2u = unpack_weight(w2_words, w2_scales, "e5m2")
    wbu = unpack_weight(wb_words, wb_scales, "e4m3")
    u = np.maximum(f64(xf)[:, idx], f64(xf)[:, idx2]) * f64(fk)
    u2 = f64(xo)[:, idx3] * sigmoid(f64(so)) * f64(fl)
    uq = mxq(u, 0, "e5m2")
    a = wu.T @ uq
    u2q = mxq(u2, 0, "e4m3")
    q = w2u.T @ u2q
    y1 = np.pad(q, ((0, 0), (1, 0)))[:, :J]
    hid = np.maximum(a, q - 0.6 * y1)
    hidq = mxq(hid, 0, "e5m2")
    p = hidq.T @ wbu
    mn = np.mean(np.abs(p), axis=1, keepdims=True)
    y = np.maximum(p - mn, 0.0) - 0.3 * f64(rs)
    return y

@@ -1,0 +1,231 @@
+from contextlib import ExitStack
+
+import concourse.mybir as mybir
+
+K, T, J, R, F, Z, N = 512, 512, 256, 512, 512, 1024, 256
+FLOPS = 2 * K * R * J + 2 * F * R * J + 2 * R * J * N
+
+F32 = mybir.dt.float32
+BF16 = mybir.dt.bfloat16
+I32 = mybir.dt.int32
+U32 = mybir.dt.uint32
+U16 = mybir.dt.uint16
+U8 = mybir.dt.uint8
+E4M3 = mybir.dt.float8_e4m3fn_x4
+E5M2 = mybir.dt.float8_e5m2_x4
+ALU = mybir.AluOpType
+ACT = mybir.ActivationFunctionType
+
+P = 128
+PACK = 4
+HALF = 128
+HALVES = J // HALF
+QUADS = 4
+
+
+def tile_list_two_largerpicks_gated_stepgap_rowabove_kernel(
+    tc, xf, fk, w_words, w_scales, xo, fl, so, w2_words, w2_scales, wb_words, wb_scales, rs, offs, offs2, offs3, out
+):
+    nc = tc.nc
+    with ExitStack() as ctx:
+        lists = ctx.enter_context(tc.tile_pool(name="lists", bufs=1))
+        sb = ctx.enter_context(tc.tile_pool(name="sb", bufs=1))
+        psum = ctx.enter_context(tc.psum_pool(name="psum", bufs=1))
+
+        def tile(shape, dtype, name):
+            return sb.tile(shape, dtype, name=name, align_bytes=64)
+
+        list1 = lists.tile([P, J // 16], U16, name="list1")
+        list2 = lists.tile([P, J // 16], U16, name="list2")
+        list3 = lists.tile([P, J // 16], U16, name="list3")
+
+        gate_in = tile([P, PACK, J], F32, "gate_in")
+        xf_pairs = [tile([P, 2, T], F32, "xf_pair%d" % i) for i in range(2)]
+        xo_planes = [tile([P, Z], F32, "xo_plane%d" % t) for t in range(PACK)]
+        fk_sb = tile([P, PACK], F32, "fk_sb")
+        fl_sb = tile([P, PACK], F32, "fl_sb")
+        w_raw = tile([P, R], U32, "w_raw")
+        w2_raw = tile([P, R], U32, "w2_raw")
+        wb_codes = tile([P, N], U32, "wb_codes")
+        w_raw_scale = tile([P, R], U8, "w_raw_scale")
+        w2_raw_scale = tile([P, R], U8, "w2_raw_scale")
+        wb_scale = tile([P, N], U8, "wb_scale")
+        rs_sb = tile([P, HALVES, N], F32, "rs_sb")
+        q_sb = tile([P, J + 1, PACK], F32, "q_sb")
+
+        def load_words(dst, words):
+            nc.sync.dma_start(out=dst[:].bitcast(I32), in_=words[0].rearrange("p n t -> p (n t)").bitcast(I32))
+
+        def load_scales(queue, dst, scales):
+            for quad in range(QUADS):
+                queue.dma_start(
+                    out=dst[32 * quad : 32 * quad + 4, :].bitcast(I32),
+                    in_=scales[0, 4 * quad : 4 * quad + 4, :].bitcast(I32),
+                )
+
+        for plane in (w2_raw_scale, w_raw_scale, wb_scale):
+            nc.gpsimd.memset(plane[:].bitcast(U32), 0)
+        nc.gpsimd.memset(q_sb[:, 0, :], 0.0)
+        load_scales(nc.gpsimd, w2_raw_scale, w2_scales)
+        load_scales(nc.gpsimd, w_raw_scale, w_scales)
+
+        xf_rows = xf.rearrange("(p t) c -> p t c", t=PACK)
+        xo_rows = xo.rearrange("(p t) c -> p t c", t=PACK)
+        nc.sync.dma_start(out=gate_in[:], in_=so.rearrange("(p t) j -> p t j", t=PACK))
+        nc.sync.dma_start(list1[:], offs)
+        nc.sync.dma_start(list2[:], offs2)
+        for i in range(2):
+            nc.sync.dma_start(out=xf_pairs[i][:], in_=xf_rows[:, 2 * i : 2 * i + 2, :])
+        nc.sync.dma_start(list3[:], offs3)
+        nc.sync.dma_start(out=fk_sb[:], in_=fk.rearrange("(p t) o -> p (t o)", t=PACK))
+        nc.sync.dma_start(out=fl_sb[:], in_=fl.rearrange("(p t) o -> p (t o)", t=PACK))
+        for t in range(PACK):
+            nc.sync.dma_start(out=xo_planes[t][:], in_=xo_rows[:, t, :])
+        load_words(w2_raw, w2_words)
+        load_words(w_raw, w_words)
+        load_words(wb_codes, wb_words)
+        nc.sync.dma_start(out=rs_sb[:], in_=rs.rearrange("(h p) n -> p h n", p=P))
+        load_scales(nc.sync, wb_scale, wb_scales)
+
+        def gather(on_vector, dst, window, offsets):
+            if on_vector:
+                nc.vector.tensor_copy(dst, window.indirect(offsets))
+            else:
+                nc.scalar.activation(dst, window.indirect(offsets), ACT.Copy)
+
+        def weave(ap):
+            return ap.rearrange("p (c i) t -> p c t i", i=4)
+
+        def planes(ap):
+            return ap.rearrange("p t (c i) -> p c t i", i=4)
+
+        gate = tile([P, PACK, J], F32, "gate")
+        nc.scalar.activation(gate[:], gate_in[:], ACT.Sigmoid)
+
+        pick1 = tile([P, PACK, J], F32, "pick1")
+        pick2 = tile([P, PACK, J], F32, "pick2")
+        larger = tile([P, PACK, J], F32, "larger")
+        for t in range(PACK):
+            window = xf_pairs[t // 2][:, t % 2, :]
+            gather(t < 3, pick1[:, t, :], window, list1[:])
+            gather(False, pick2[:, t, :], window, list2[:])
+            nc.vector.tensor_tensor(larger[:, t, :], pick1[:, t, :], pick2[:, t, :], ALU.max)
+        u_bf = tile([P, J, PACK], BF16, "u_bf")
+        nc.vector.tensor_tensor(
+            weave(u_bf[:]),
+            planes(larger[:]),
+            fk_sb[:].unsqueeze(1).unsqueeze(3).to_broadcast([P, J // 4, PACK, 4]),
+            ALU.mult,
+        )
+        u_codes = tile([P, J], U32, "u_codes")
+        u_scale = tile([P, J], U8, "u_scale")
+        nc.vector.quantize_mx(out=u_codes[:].bitcast(E5M2), scales=u_scale[:], in_=u_bf[:].rearrange("p j t -> p (j t)"))
+
+        w_scale = tile([P, R], U8, "w_scale")
+        w2_scale = tile([P, R], U8, "w2_scale")
+        for dst, src in ((w2_scale, w2_raw_scale), (w_scale, w_raw_scale)):
+            nc.vector.tensor_copy(
+                dst[:].rearrange("p (t c i) -> p c t i", t=PACK, i=16),
+                src[:].rearrange("p (c i t) -> p c t i", t=PACK, i=16),
+            )
+
+        pick3 = tile([P, PACK, J], F32, "pick3")
+        u2_planes = tile([P, PACK, J], BF16, "u2_planes")
+
+        def gated(t, cols):
+            nc.vector.scalar_tensor_tensor(
+                u2_planes[:, t, cols], pick3[:, t, cols], fl_sb[:, t : t + 1], gate[:, t, cols], ALU.mult, ALU.mult
+            )
+
+        for t in range(PACK - 1):
+            gather(False, pick3[:, t, :], xo_planes[t][:], list3[:])
+            gated(t, slice(0, J))
+        last = PACK - 1
+        for h in range(HALVES):
+            cols = slice(h * HALF, (h + 1) * HALF)
+            gather(h == 0, pick3[:, last, cols], xo_planes[last][:], list3[:, h * 8 : (h + 1) * 8])
+        for h in range(HALVES):
+            gated(last, slice(h * HALF, (h + 1) * HALF))
+
+        w_codes = tile([P, R], U32, "w_codes")
+        w2_codes = tile([P, R], U32, "w2_codes")
+
+        def deal_words(dst, src):
+            nc.scalar.copy(
+                dst[:].rearrange("p (t c i) -> p c t i", t=PACK, i=4),
+                src[:].rearrange("p (c i t) -> p c t i", t=PACK, i=4),
+            )
+
+        deal_words(w2_codes, w2_raw)
+        u2_bf = [tile([P, HALF, PACK], BF16, "u2_bf%d" % h) for h in range(HALVES)]
+        u2_codes = [tile([P, HALF], U32, "u2_codes%d" % h) for h in range(HALVES)]
+        u2_scale = [tile([P, HALF], U8, "u2_scale%d" % h) for h in range(HALVES)]
+        nc.vector.tensor_copy(weave(u2_bf[0][:]), planes(u2_planes[:, :, 0:HALF]))
+        nc.scalar.copy(weave(u2_bf[1][:]), planes(u2_planes[:, :, HALF:J]))
+        deal_words(w_codes, w_raw)
+
+        q_ps = [psum.tile([P, PACK, HALF], F32, name="q_ps%d" % h) for h in range(HALVES)]
+        a_ps = [psum.tile([P, PACK, HALF], F32, name="a_ps%d" % h) for h in range(HALVES)]
+        p_ps = [psum.tile([P, N], F32, name="p_ps%d" % h) for h in range(HALVES)]
+
+        def first_stage(acc, codes, scale, rhs, rhs_scale):
+            for t in range(PACK):
+                cols = slice(t * P, (t + 1) * P)
+                nc.tensor.matmul_mx(
+                    out=acc[:, t, :],
+                    lhsT=codes[:, cols].bitcast(E5M2),
+                    lhsT_scale=scale[:, cols],
+                    rhs=rhs,
+                    rhs_scale=rhs_scale,
+                    start=True,
+                    stop=True,
+                )
+
+        for h in range(HALVES):
+            nc.vector.quantize_mx(
+                out=u2_codes[h][:].bitcast(E4M3), scales=u2_scale[h][:], in_=u2_bf[h][:].rearrange("p j t -> p (j t)")
+            )
+            first_stage(q_ps[h], w2_codes, w2_scale, u2_codes[h][:].bitcast(E4M3), u2_scale[h][:])
+        for h in range(HALVES):
+            cols = slice(h * HALF, (h + 1) * HALF)
+            first_stage(a_ps[h], w_codes, w_scale, u_codes[:, cols].bitcast(E5M2), u_scale[:, cols])
+
+        step = [tile([P, HALF, PACK], F32, "step%d" % h) for h in range(HALVES)]
+        hid_bf = [tile([P, HALF, PACK], BF16, "hid_bf%d" % h) for h in range(HALVES)]
+        hid_codes = [tile([P, HALF], U32, "hid_codes%d" % h) for h in range(HALVES)]
+        hid_scale = [tile([P, HALF], U8, "hid_scale%d" % h) for h in range(HALVES)]
+        for h in range(HALVES):
+            nc.scalar.copy(q_sb[:, 1 + h * HALF : 1 + (h + 1) * HALF, :], q_ps[h][:].rearrange("p t j -> p j t"))
+        for h in range(HALVES):
+            nc.vector.scalar_tensor_tensor(
+                step[h][:],
+                q_sb[:, h * HALF : (h + 1) * HALF, :],
+                -0.6,
+                q_ps[h][:].rearrange("p t j -> p j t"),
+                ALU.mult,
+                ALU.add,
+            )
+            nc.vector.tensor_tensor(hid_bf[h][:], step[h][:], a_ps[h][:].rearrange("p t j -> p j t"), ALU.max)
+        for h in range(HALVES):
+            nc.vector.quantize_mx(
+                out=hid_codes[h][:].bitcast(E5M2), scales=hid_scale[h][:], in_=hid_bf[h][:].rearrange("p j t -> p (j t)")
+            )
+            nc.tensor.matmul_mx(
+                out=p_ps[h][:],
+                lhsT=hid_codes[h][:].bitcast(E5M2),
+                lhsT_scale=hid_scale[h][:],
+                rhs=wb_codes[:].bitcast(E4M3),
+                rhs_scale=wb_scale[:],
+                start=True,
+                stop=True,
+            )
+
+        for h in range(HALVES):
+            magnitude = tile([P, N], F32, "magnitude%d" % h)
+            mean = tile([P, 1], F32, "mean%d" % h)
+            above = tile([P, N], F32, "above%d" % h)
+            result = tile([P, N], F32, "result%d" % h)
+            nc.scalar.activation(magnitude[:], p_ps[h][:], ACT.Abs, scale=1.0 / N, accum_out=mean[:])
+            nc.vector.tensor_scalar(above[:], p_ps[h][:], mean[:], 0.0, ALU.subtract, ALU.max)
+            nc.vector.scalar_tensor_tensor(result[:], rs_sb[:, h, :], -0.3, above[:], ALU.mult, ALU.add)
+            nc.sync.dma_start(out=out[h * HALF : (h + 1) * HALF, :], in_=result[:])

@@ -32,60 +32,53 @@ def tile_list_two_largerpicks_gated_stepgap_rowabove_kernel(
         sb = ctx.enter_context(tc.tile_pool(name="sb", bufs=1))
         psum = ctx.enter_context(tc.psum_pool(name="psum", bufs=1))
 
-        def tile(shape, dtype, name):
-            return sb.tile(shape, dtype, name=name, align_bytes=64)
+        def tile(shape, dtype, name, tag=None):
+            return sb.tile(shape, dtype, name=name, tag=tag or name, align_bytes=64)
 
         list1 = lists.tile([P, J // 16], U16, name="list1")
         list2 = lists.tile([P, J // 16], U16, name="list2")
         list3 = lists.tile([P, J // 16], U16, name="list3")
 
-        gate_in = tile([P, PACK, J], F32, "gate_in")
-        xf_pairs = [tile([P, 2, T], F32, "xf_pair%d" % i) for i in range(2)]
-        xo_planes = [tile([P, Z], F32, "xo_plane%d" % t) for t in range(PACK)]
+        gate_first = tile([P, J], F32, "gate_first")
+        gate_rest = tile([P, PACK - 1, J], F32, "gate_rest")
+        xf_0 = tile([P, T], F32, "xf_0")
+        xf_1 = tile([P, T], F32, "xf_1")
+        xf_23 = tile([P, 2, T], F32, "xf_23")
+        xo_planes = [tile([P, Z], F32, "xo_plane%d" % t) for t in range(PACK - 1)]
         fk_sb = tile([P, PACK], F32, "fk_sb")
         fl_sb = tile([P, PACK], F32, "fl_sb")
-        w_raw = tile([P, R], U32, "w_raw")
-        w2_raw = tile([P, R], U32, "w2_raw")
-        wb_codes = tile([P, N], U32, "wb_codes")
-        w_raw_scale = tile([P, R], U8, "w_raw_scale")
         w2_raw_scale = tile([P, R], U8, "w2_raw_scale")
-        wb_scale = tile([P, N], U8, "wb_scale")
-        rs_sb = tile([P, HALVES, N], F32, "rs_sb")
         q_sb = tile([P, J + 1, PACK], F32, "q_sb")
 
         def load_words(dst, words):
             nc.sync.dma_start(out=dst[:].bitcast(I32), in_=words[0].rearrange("p n t -> p (n t)").bitcast(I32))
 
-        def load_scales(queue, dst, scales):
+        def load_scales(dst, scales):
+            nc.gpsimd.memset(dst[:].bitcast(U32), 0)
             for quad in range(QUADS):
-                queue.dma_start(
+                nc.sync.dma_start(
                     out=dst[32 * quad : 32 * quad + 4, :].bitcast(I32),
                     in_=scales[0, 4 * quad : 4 * quad + 4, :].bitcast(I32),
                 )
 
-        for plane in (w2_raw_scale, w_raw_scale, wb_scale):
-            nc.gpsimd.memset(plane[:].bitcast(U32), 0)
         nc.gpsimd.memset(q_sb[:, 0, :], 0.0)
-        load_scales(nc.gpsimd, w2_raw_scale, w2_scales)
-        load_scales(nc.gpsimd, w_raw_scale, w_scales)
 
         xf_rows = xf.rearrange("(p t) c -> p t c", t=PACK)
         xo_rows = xo.rearrange("(p t) c -> p t c", t=PACK)
-        nc.sync.dma_start(out=gate_in[:], in_=so.rearrange("(p t) j -> p t j", t=PACK))
+        so_rows = so.rearrange("(p t) j -> p t j", t=PACK)
+        nc.sync.dma_start(out=gate_first[:], in_=so_rows[:, 0, :])
         nc.sync.dma_start(list1[:], offs)
         nc.sync.dma_start(list2[:], offs2)
-        for i in range(2):
-            nc.sync.dma_start(out=xf_pairs[i][:], in_=xf_rows[:, 2 * i : 2 * i + 2, :])
-        nc.sync.dma_start(list3[:], offs3)
+        nc.sync.dma_start(out=xf_0[:], in_=xf_rows[:, 0, :])
+        nc.sync.dma_start(out=xf_1[:], in_=xf_rows[:, 1, :])
+        nc.sync.dma_start(out=xf_23[:], in_=xf_rows[:, 2:4, :])
         nc.sync.dma_start(out=fk_sb[:], in_=fk.rearrange("(p t) o -> p (t o)", t=PACK))
+        nc.sync.dma_start(out=gate_rest[:], in_=so_rows[:, 1:PACK, :])
+        nc.sync.dma_start(list3[:], offs3)
         nc.sync.dma_start(out=fl_sb[:], in_=fl.rearrange("(p t) o -> p (t o)", t=PACK))
-        for t in range(PACK):
+        for t in range(PACK - 1):
             nc.sync.dma_start(out=xo_planes[t][:], in_=xo_rows[:, t, :])
-        load_words(w2_raw, w2_words)
-        load_words(w_raw, w_words)
-        load_words(wb_codes, wb_words)
-        nc.sync.dma_start(out=rs_sb[:], in_=rs.rearrange("(h p) n -> p h n", p=P))
-        load_scales(nc.sync, wb_scale, wb_scales)
+        load_scales(w2_raw_scale, w2_scales)
 
         def gather(on_vector, dst, window, offsets):
             if on_vector:
@@ -100,16 +93,31 @@ def tile_list_two_largerpicks_gated_stepgap_rowabove_kernel(
             return ap.rearrange("p t (c i) -> p c t i", i=4)
 
         gate = tile([P, PACK, J], F32, "gate")
-        nc.scalar.activation(gate[:], gate_in[:], ACT.Sigmoid)
+        nc.scalar.activation(gate[:, 0, :], gate_first[:], ACT.Sigmoid)
+
+        xo_last = tile([P, Z], F32, "xo_last", tag="gate_first")
+        xo_planes.append(xo_last)
+        nc.sync.dma_start(out=xo_last[:], in_=xo_rows[:, PACK - 1, :])
 
         pick1 = tile([P, PACK, J], F32, "pick1")
         pick2 = tile([P, PACK, J], F32, "pick2")
         larger = tile([P, PACK, J], F32, "larger")
         for t in range(PACK):
-            window = xf_pairs[t // 2][:, t % 2, :]
+            window = (xf_0[:], xf_1[:], xf_23[:, 0, :], xf_23[:, 1, :])[t]
             gather(t < 3, pick1[:, t, :], window, list1[:])
             gather(False, pick2[:, t, :], window, list2[:])
             nc.vector.tensor_tensor(larger[:, t, :], pick1[:, t, :], pick2[:, t, :], ALU.max)
+        nc.scalar.activation(gate[:, 1:PACK, :], gate_rest[:], ACT.Sigmoid)
+        w2_raw = tile([P, R], U32, "w2_raw", tag="xf_0")
+        load_words(w2_raw, w2_words)
+        w_raw = tile([P, R], U32, "w_raw", tag="xf_1")
+        load_words(w_raw, w_words)
+        w_raw_scale = tile([P, R], U8, "w_raw_scale", tag="xf_23")
+        load_scales(w_raw_scale, w_scales)
+        wb_codes = tile([P, N], U32, "wb_codes", tag="gate_rest")
+        load_words(wb_codes, wb_words)
+        rs_sb = tile([P, HALVES, N], F32, "rs_sb", tag="pick1")
+        nc.sync.dma_start(out=rs_sb[:], in_=rs.rearrange("(h p) n -> p h n", p=P))
         u_bf = tile([P, J, PACK], BF16, "u_bf")
         nc.vector.tensor_tensor(
             weave(u_bf[:]),
@@ -117,38 +125,33 @@ def tile_list_two_largerpicks_gated_stepgap_rowabove_kernel(
             fk_sb[:].unsqueeze(1).unsqueeze(3).to_broadcast([P, J // 4, PACK, 4]),
             ALU.mult,
         )
+        wb_scale = tile([P, N], U8, "wb_scale", tag="pick2")
+        load_scales(wb_scale, wb_scales)
         u_codes = tile([P, J], U32, "u_codes")
         u_scale = tile([P, J], U8, "u_scale")
         nc.vector.quantize_mx(out=u_codes[:].bitcast(E5M2), scales=u_scale[:], in_=u_bf[:].rearrange("p j t -> p (j t)"))
 
-        w_scale = tile([P, R], U8, "w_scale")
-        w2_scale = tile([P, R], U8, "w2_scale")
-        for dst, src in ((w2_scale, w2_raw_scale), (w_scale, w_raw_scale)):
+        def deal_scales(dst, src):
             nc.vector.tensor_copy(
                 dst[:].rearrange("p (t c i) -> p c t i", t=PACK, i=16),
                 src[:].rearrange("p (c i t) -> p c t i", t=PACK, i=16),
             )
 
+        factor = tile([P, PACK, J], F32, "factor", tag="larger")
+        for t in range(PACK):
+            nc.vector.tensor_scalar(factor[:, t, :], gate[:, t, :], fl_sb[:, t : t + 1], None, ALU.mult)
+        w2_scale = tile([P, R], U8, "w2_scale", tag="u_bf")
+        deal_scales(w2_scale, w2_raw_scale)
+
         pick3 = tile([P, PACK, J], F32, "pick3")
-        u2_planes = tile([P, PACK, J], BF16, "u2_planes")
-
-        def gated(t, cols):
-            nc.vector.scalar_tensor_tensor(
-                u2_planes[:, t, cols], pick3[:, t, cols], fl_sb[:, t : t + 1], gate[:, t, cols], ALU.mult, ALU.mult
-            )
-
         for t in range(PACK - 1):
             gather(False, pick3[:, t, :], xo_planes[t][:], list3[:])
-            gated(t, slice(0, J))
         last = PACK - 1
         for h in range(HALVES):
             cols = slice(h * HALF, (h + 1) * HALF)
             gather(h == 0, pick3[:, last, cols], xo_planes[last][:], list3[:, h * 8 : (h + 1) * 8])
-        for h in range(HALVES):
-            gated(last, slice(h * HALF, (h + 1) * HALF))
 
-        w_codes = tile([P, R], U32, "w_codes")
-        w2_codes = tile([P, R], U32, "w2_codes")
+        w2_codes = tile([P, R], U32, "w2_codes", tag="gate_first")
 
         def deal_words(dst, src):
             nc.scalar.copy(
@@ -157,11 +160,9 @@ def tile_list_two_largerpicks_gated_stepgap_rowabove_kernel(
             )
 
         deal_words(w2_codes, w2_raw)
-        u2_bf = [tile([P, HALF, PACK], BF16, "u2_bf%d" % h) for h in range(HALVES)]
         u2_codes = [tile([P, HALF], U32, "u2_codes%d" % h) for h in range(HALVES)]
         u2_scale = [tile([P, HALF], U8, "u2_scale%d" % h) for h in range(HALVES)]
-        nc.vector.tensor_copy(weave(u2_bf[0][:]), planes(u2_planes[:, :, 0:HALF]))
-        nc.scalar.copy(weave(u2_bf[1][:]), planes(u2_planes[:, :, HALF:J]))
+        w_codes = tile([P, R], U32, "w_codes", tag="xf_0")
         deal_words(w_codes, w_raw)
 
         q_ps = [psum.tile([P, PACK, HALF], F32, name="q_ps%d" % h) for h in range(HALVES)]
@@ -182,36 +183,40 @@ def tile_list_two_largerpicks_gated_stepgap_rowabove_kernel(
                 )
 
         for h in range(HALVES):
+            cols = slice(h * HALF, (h + 1) * HALF)
+            u2_bf = tile([P, HALF, PACK], BF16, "u2_bf")
+            nc.vector.tensor_tensor(weave(u2_bf[:]), planes(pick3[:, :, cols]), planes(factor[:, :, cols]), ALU.mult)
             nc.vector.quantize_mx(
-                out=u2_codes[h][:].bitcast(E4M3), scales=u2_scale[h][:], in_=u2_bf[h][:].rearrange("p j t -> p (j t)")
+                out=u2_codes[h][:].bitcast(E4M3), scales=u2_scale[h][:], in_=u2_bf[:].rearrange("p j t -> p (j t)")
             )
             first_stage(q_ps[h], w2_codes, w2_scale, u2_codes[h][:].bitcast(E4M3), u2_scale[h][:])
+        w_scale = tile([P, R], U8, "w_scale", tag="u2_bf")
+        deal_scales(w_scale, w_raw_scale)
         for h in range(HALVES):
             cols = slice(h * HALF, (h + 1) * HALF)
             first_stage(a_ps[h], w_codes, w_scale, u_codes[:, cols].bitcast(E5M2), u_scale[:, cols])
 
-        step = [tile([P, HALF, PACK], F32, "step%d" % h) for h in range(HALVES)]
-        hid_bf = [tile([P, HALF, PACK], BF16, "hid_bf%d" % h) for h in range(HALVES)]
+        steps = tile([P, J, PACK], F32, "steps", tag="xf_23")
+        step = [steps[:, h * HALF : (h + 1) * HALF, :] for h in range(HALVES)]
         hid_codes = [tile([P, HALF], U32, "hid_codes%d" % h) for h in range(HALVES)]
         hid_scale = [tile([P, HALF], U8, "hid_scale%d" % h) for h in range(HALVES)]
         for h in range(HALVES):
             nc.scalar.copy(q_sb[:, 1 + h * HALF : 1 + (h + 1) * HALF, :], q_ps[h][:].rearrange("p t j -> p j t"))
         for h in range(HALVES):
             nc.vector.scalar_tensor_tensor(
-                step[h][:],
+                step[h],
                 q_sb[:, h * HALF : (h + 1) * HALF, :],
                 -0.6,
                 q_ps[h][:].rearrange("p t j -> p j t"),
                 ALU.mult,
                 ALU.add,
             )
-            nc.vector.tensor_tensor(hid_bf[h][:], step[h][:], a_ps[h][:].rearrange("p t j -> p j t"), ALU.max)
-        for h in range(HALVES):
-            nc.vector.quantize_mx(
-                out=hid_codes[h][:].bitcast(E5M2), scales=hid_scale[h][:], in_=hid_bf[h][:].rearrange("p j t -> p (j t)")
-            )
+        rs_scaled = tile([P, HALVES, N], F32, "rs_scaled", tag="xf_1")
+        nc.scalar.activation(rs_scaled[:], rs_sb[:], ACT.Copy, scale=-0.3)
+
+        def second_stage(acc, h):
             nc.tensor.matmul_mx(
-                out=p_ps[h][:],
+                out=acc[:],
                 lhsT=hid_codes[h][:].bitcast(E5M2),
                 lhsT_scale=hid_scale[h][:],
                 rhs=wb_codes[:].bitcast(E4M3),
@@ -220,12 +225,24 @@ def tile_list_two_largerpicks_gated_stepgap_rowabove_kernel(
                 stop=True,
             )
 
+        p_twin = psum.tile([P, N], F32, name="p_twin")
+        for h in range(HALVES):
+            hid_bf = tile([P, HALF, PACK], BF16, "hid_bf")
+            nc.vector.tensor_tensor(hid_bf[:], step[h], a_ps[h][:].rearrange("p t j -> p j t"), ALU.max)
+            nc.vector.quantize_mx(
+                out=hid_codes[h][:].bitcast(E5M2), scales=hid_scale[h][:], in_=hid_bf[:].rearrange("p j t -> p (j t)")
+            )
+            if h == HALVES - 1:
+                second_stage(p_twin, h)
+            second_stage(p_ps[h], h)
+
         for h in range(HALVES):
             magnitude = tile([P, N], F32, "magnitude%d" % h)
             mean = tile([P, 1], F32, "mean%d" % h)
-            above = tile([P, N], F32, "above%d" % h)
+            shifted = tile([P, N], F32, "shifted%d" % h)
             result = tile([P, N], F32, "result%d" % h)
-            nc.scalar.activation(magnitude[:], p_ps[h][:], ACT.Abs, scale=1.0 / N, accum_out=mean[:])
-            nc.vector.tensor_scalar(above[:], p_ps[h][:], mean[:], 0.0, ALU.subtract, ALU.max)
-            nc.vector.scalar_tensor_tensor(result[:], rs_sb[:, h, :], -0.3, above[:], ALU.mult, ALU.add)
+            source = p_twin if h == HALVES - 1 else p_ps[h]
+            nc.scalar.activation(magnitude[:], source[:], ACT.Abs, scale=1.0 / N, accum_out=mean[:])
+            nc.vector.tensor_tensor(shifted[:], p_ps[h][:], rs_scaled[:, h, :], ALU.add)
+            nc.vector.scalar_tensor_tensor(result[:], shifted[:], mean[:], rs_scaled[:, h, :], ALU.subtract, ALU.max)
             nc.sync.dma_start(out=out[h * HALF : (h + 1) * HALF, :], in_=result[:])

@@ -21,6 +21,7 @@ PACK = 4
 HALF = 128
 HALVES = J // HALF
 QUADS = 4
+LEAD = 4
 
 
 def tile_list_two_largerpicks_gated_stepgap_rowabove_kernel(
@@ -44,11 +45,12 @@ def tile_list_two_largerpicks_gated_stepgap_rowabove_kernel(
         xf_0 = tile([P, T], F32, "xf_0")
         xf_1 = tile([P, T], F32, "xf_1")
         xf_23 = tile([P, 2, T], F32, "xf_23")
-        xo_planes = [tile([P, Z], F32, "xo_plane%d" % t) for t in range(PACK - 1)]
+        xo_01 = tile([P, 2, Z], F32, "xo_01")
+        xo_2 = tile([P, Z], F32, "xo_2")
         fk_sb = tile([P, PACK], F32, "fk_sb")
         fl_sb = tile([P, PACK], F32, "fl_sb")
         w2_raw_scale = tile([P, R], U8, "w2_raw_scale")
-        q_sb = tile([P, J + 1, PACK], F32, "q_sb")
+        q_sb = tile([P, PACK, LEAD + J], F32, "q_sb")
 
         def load_words(dst, words):
             nc.sync.dma_start(out=dst[:].bitcast(I32), in_=words[0].rearrange("p n t -> p (n t)").bitcast(I32))
@@ -61,7 +63,7 @@ def tile_list_two_largerpicks_gated_stepgap_rowabove_kernel(
                     in_=scales[0, 4 * quad : 4 * quad + 4, :].bitcast(I32),
                 )
 
-        nc.gpsimd.memset(q_sb[:, 0, :], 0.0)
+        nc.gpsimd.memset(q_sb[:, :, 0:LEAD], 0.0)
 
         xf_rows = xf.rearrange("(p t) c -> p t c", t=PACK)
         xo_rows = xo.rearrange("(p t) c -> p t c", t=PACK)
@@ -76,8 +78,8 @@ def tile_list_two_largerpicks_gated_stepgap_rowabove_kernel(
         nc.sync.dma_start(out=gate_rest[:], in_=so_rows[:, 1:PACK, :])
         nc.sync.dma_start(list3[:], offs3)
         nc.sync.dma_start(out=fl_sb[:], in_=fl.rearrange("(p t) o -> p (t o)", t=PACK))
-        for t in range(PACK - 1):
-            nc.sync.dma_start(out=xo_planes[t][:], in_=xo_rows[:, t, :])
+        nc.sync.dma_start(out=xo_01[:], in_=xo_rows[:, 0:2, :])
+        nc.sync.dma_start(out=xo_2[:], in_=xo_rows[:, 2, :])
         load_scales(w2_raw_scale, w2_scales)
 
         def gather(on_vector, dst, window, offsets):
@@ -96,7 +98,6 @@ def tile_list_two_largerpicks_gated_stepgap_rowabove_kernel(
         nc.scalar.activation(gate[:, 0, :], gate_first[:], ACT.Sigmoid)
 
         xo_last = tile([P, Z], F32, "xo_last", tag="gate_first")
-        xo_planes.append(xo_last)
         nc.sync.dma_start(out=xo_last[:], in_=xo_rows[:, PACK - 1, :])
 
         pick1 = tile([P, PACK, J], F32, "pick1")
@@ -145,11 +146,11 @@ def tile_list_two_largerpicks_gated_stepgap_rowabove_kernel(
 
         pick3 = tile([P, PACK, J], F32, "pick3")
         for t in range(PACK - 1):
-            gather(False, pick3[:, t, :], xo_planes[t][:], list3[:])
+            gather(False, pick3[:, t, :], (xo_01[:, 0, :], xo_01[:, 1, :], xo_2[:])[t], list3[:])
         last = PACK - 1
         for h in range(HALVES):
             cols = slice(h * HALF, (h + 1) * HALF)
-            gather(h == 0, pick3[:, last, cols], xo_planes[last][:], list3[:, h * 8 : (h + 1) * 8])
+            gather(h == 0, pick3[:, last, cols], xo_last[:], list3[:, h * 8 : (h + 1) * 8])
 
         w2_codes = tile([P, R], U32, "w2_codes", tag="gate_first")
 
@@ -165,84 +166,84 @@ def tile_list_two_largerpicks_gated_stepgap_rowabove_kernel(
         w_codes = tile([P, R], U32, "w_codes", tag="xf_0")
         deal_words(w_codes, w_raw)
 
-        q_ps = [psum.tile([P, PACK, HALF], F32, name="q_ps%d" % h) for h in range(HALVES)]
+        q_ps = [[psum.tile([P, 2, HALF], F32, name="q_ps%d%d" % (h, u)) for u in range(2)] for h in range(HALVES)]
         a_ps = [psum.tile([P, PACK, HALF], F32, name="a_ps%d" % h) for h in range(HALVES)]
         p_ps = [psum.tile([P, N], F32, name="p_ps%d" % h) for h in range(HALVES)]
 
-        def first_stage(acc, codes, scale, rhs, rhs_scale):
-            for t in range(PACK):
-                cols = slice(t * P, (t + 1) * P)
-                nc.tensor.matmul_mx(
-                    out=acc[:, t, :],
-                    lhsT=codes[:, cols].bitcast(E5M2),
-                    lhsT_scale=scale[:, cols],
-                    rhs=rhs,
-                    rhs_scale=rhs_scale,
-                    start=True,
-                    stop=True,
-                )
-
-        for h in range(HALVES):
-            cols = slice(h * HALF, (h + 1) * HALF)
-            u2_bf = tile([P, HALF, PACK], BF16, "u2_bf")
-            nc.vector.tensor_tensor(weave(u2_bf[:]), planes(pick3[:, :, cols]), planes(factor[:, :, cols]), ALU.mult)
-            nc.vector.quantize_mx(
-                out=u2_codes[h][:].bitcast(E4M3), scales=u2_scale[h][:], in_=u2_bf[:].rearrange("p j t -> p (j t)")
-            )
-            first_stage(q_ps[h], w2_codes, w2_scale, u2_codes[h][:].bitcast(E4M3), u2_scale[h][:])
-        w_scale = tile([P, R], U8, "w_scale", tag="u2_bf")
-        deal_scales(w_scale, w_raw_scale)
-        for h in range(HALVES):
-            cols = slice(h * HALF, (h + 1) * HALF)
-            first_stage(a_ps[h], w_codes, w_scale, u_codes[:, cols].bitcast(E5M2), u_scale[:, cols])
-
-        steps = tile([P, J, PACK], F32, "steps", tag="xf_23")
-        step = [steps[:, h * HALF : (h + 1) * HALF, :] for h in range(HALVES)]
-        hid_codes = [tile([P, HALF], U32, "hid_codes%d" % h) for h in range(HALVES)]
-        hid_scale = [tile([P, HALF], U8, "hid_scale%d" % h) for h in range(HALVES)]
-        for h in range(HALVES):
-            nc.scalar.copy(q_sb[:, 1 + h * HALF : 1 + (h + 1) * HALF, :], q_ps[h][:].rearrange("p t j -> p j t"))
-        for h in range(HALVES):
-            nc.vector.scalar_tensor_tensor(
-                step[h],
-                q_sb[:, h * HALF : (h + 1) * HALF, :],
-                -0.6,
-                q_ps[h][:].rearrange("p t j -> p j t"),
-                ALU.mult,
-                ALU.add,
-            )
-        rs_scaled = tile([P, HALVES, N], F32, "rs_scaled", tag="xf_1")
-        nc.scalar.activation(rs_scaled[:], rs_sb[:], ACT.Copy, scale=-0.3)
-
-        def second_stage(acc, h):
+        def first_stage(acc, t, codes, scale, rhs, rhs_scale):
+            cols = slice(t * P, (t + 1) * P)
             nc.tensor.matmul_mx(
-                out=acc[:],
-                lhsT=hid_codes[h][:].bitcast(E5M2),
-                lhsT_scale=hid_scale[h][:],
-                rhs=wb_codes[:].bitcast(E4M3),
-                rhs_scale=wb_scale[:],
+                out=acc,
+                lhsT=codes[:, cols].bitcast(E5M2),
+                lhsT_scale=scale[:, cols],
+                rhs=rhs,
+                rhs_scale=rhs_scale,
                 start=True,
                 stop=True,
             )
 
-        p_twin = psum.tile([P, N], F32, name="p_twin")
+        u2_bf = [tile([P, HALF, PACK], BF16, "u2_bf%d" % h, tag=("u2_bf0", "u2_bf1")[h]) for h in range(HALVES)]
         for h in range(HALVES):
-            hid_bf = tile([P, HALF, PACK], BF16, "hid_bf")
-            nc.vector.tensor_tensor(hid_bf[:], step[h], a_ps[h][:].rearrange("p t j -> p j t"), ALU.max)
+            cols = slice(h * HALF, (h + 1) * HALF)
+            nc.vector.tensor_tensor(weave(u2_bf[h][:]), planes(pick3[:, :, cols]), planes(factor[:, :, cols]), ALU.mult)
             nc.vector.quantize_mx(
-                out=hid_codes[h][:].bitcast(E5M2), scales=hid_scale[h][:], in_=hid_bf[:].rearrange("p j t -> p (j t)")
+                out=u2_codes[h][:].bitcast(E4M3), scales=u2_scale[h][:], in_=u2_bf[h][:].rearrange("p j t -> p (j t)")
             )
-            if h == HALVES - 1:
-                second_stage(p_twin, h)
-            second_stage(p_ps[h], h)
+            for t in range(PACK):
+                first_stage(q_ps[h][t // 2][:, t % 2, :], t, w2_codes, w2_scale, u2_codes[h][:].bitcast(E4M3), u2_scale[h][:])
+        w_scale = tile([P, R], U8, "w_scale", tag="u2_bf1")
+        deal_scales(w_scale, w_raw_scale)
+        for h in range(HALVES):
+            cols = slice(h * HALF, (h + 1) * HALF)
+            for t in range(PACK):
+                first_stage(a_ps[h][:, t, :], t, w_codes, w_scale, u_codes[:, cols].bitcast(E5M2), u_scale[:, cols])
+
+        steps = tile([P, PACK, J], F32, "steps", tag="xf_23")
+        for h in range(HALVES):
+            for u in range(2):
+                nc.scalar.copy(q_sb[:, 2 * u : 2 * u + 2, LEAD + h * HALF : LEAD + (h + 1) * HALF], q_ps[h][u][:])
+
+        rs_scaled = tile([P, HALVES, N], F32, "rs_scaled", tag="u2_codes1")
+        nc.scalar.activation(rs_scaled[:], rs_sb[:], ACT.Copy, scale=-0.3)
+
+        p_twin = []
+        for h in range(HALVES):
+            cols = slice(h * HALF, (h + 1) * HALF)
+            for u in range(2):
+                nc.vector.scalar_tensor_tensor(
+                    steps[:, 2 * u : 2 * u + 2, cols],
+                    q_sb[:, 2 * u : 2 * u + 2, LEAD - 1 + h * HALF : LEAD - 1 + (h + 1) * HALF],
+                    -0.6,
+                    q_ps[h][u][:],
+                    ALU.mult,
+                    ALU.add,
+                )
+            hid_bf = tile([P, HALF, PACK], BF16, "hid_bf%d" % h)
+            hid_codes = tile([P, HALF], U32, "hid_codes%d" % h)
+            hid_scale = tile([P, HALF], U8, "hid_scale%d" % h)
+            nc.vector.tensor_tensor(weave(hid_bf[:]), planes(steps[:, :, cols]), planes(a_ps[h][:]), ALU.max)
+            nc.vector.quantize_mx(
+                out=hid_codes[:].bitcast(E5M2), scales=hid_scale[:], in_=hid_bf[:].rearrange("p j t -> p (j t)")
+            )
+            twin = psum.tile([P, N], F32, name="p_twin%d" % h, tag="q_ps0%d" % h)
+            p_twin.append(twin)
+            for acc in (twin, p_ps[h]):
+                nc.tensor.matmul_mx(
+                    out=acc[:],
+                    lhsT=hid_codes[:].bitcast(E5M2),
+                    lhsT_scale=hid_scale[:],
+                    rhs=wb_codes[:].bitcast(E4M3),
+                    rhs_scale=wb_scale[:],
+                    start=True,
+                    stop=True,
+                )
 
         for h in range(HALVES):
             magnitude = tile([P, N], F32, "magnitude%d" % h)
             mean = tile([P, 1], F32, "mean%d" % h)
             shifted = tile([P, N], F32, "shifted%d" % h)
             result = tile([P, N], F32, "result%d" % h)
-            source = p_twin if h == HALVES - 1 else p_ps[h]
-            nc.scalar.activation(magnitude[:], source[:], ACT.Abs, scale=1.0 / N, accum_out=mean[:])
+            nc.scalar.activation(magnitude[:], p_twin[h][:], ACT.Abs, scale=1.0 / N, accum_out=mean[:])
             nc.vector.tensor_tensor(shifted[:], p_ps[h][:], rs_scaled[:, h, :], ALU.add)
             nc.vector.scalar_tensor_tensor(result[:], shifted[:], mean[:], rs_scaled[:, h, :], ALU.subtract, ALU.max)
             nc.sync.dma_start(out=out[h * HALF : (h + 1) * HALF, :], in_=result[:])

from contextlib import ExitStack

import concourse.mybir as mybir

K, T, J, R, F, Z, N = 512, 512, 256, 512, 512, 1024, 256
FLOPS = 2 * K * R * J + 2 * F * R * J + 2 * R * J * N

F32 = mybir.dt.float32
BF16 = mybir.dt.bfloat16
I32 = mybir.dt.int32
U32 = mybir.dt.uint32
U16 = mybir.dt.uint16
U8 = mybir.dt.uint8
E4M3 = mybir.dt.float8_e4m3fn_x4
E5M2 = mybir.dt.float8_e5m2_x4
ALU = mybir.AluOpType
ACT = mybir.ActivationFunctionType

P = 128
PACK = 4
HALF = 128
HALVES = J // HALF
QUADS = 4
LEAD = 4


def tile_list_two_largerpicks_gated_stepgap_rowabove_kernel(
    tc, xf, fk, w_words, w_scales, xo, fl, so, w2_words, w2_scales, wb_words, wb_scales, rs, offs, offs2, offs3, out
):
    nc = tc.nc
    with ExitStack() as ctx:
        lists = ctx.enter_context(tc.tile_pool(name="lists", bufs=1))
        sb = ctx.enter_context(tc.tile_pool(name="sb", bufs=1))
        psum = ctx.enter_context(tc.psum_pool(name="psum", bufs=1))

        def tile(shape, dtype, name, tag=None):
            return sb.tile(shape, dtype, name=name, tag=tag or name, align_bytes=64)

        list1 = lists.tile([P, J // 16], U16, name="list1")
        list2 = lists.tile([P, J // 16], U16, name="list2")
        list3 = lists.tile([P, J // 16], U16, name="list3")

        gate_first = tile([P, J], F32, "gate_first")
        gate_rest = tile([P, PACK - 1, J], F32, "gate_rest")
        xf_0 = tile([P, T], F32, "xf_0")
        xf_1 = tile([P, T], F32, "xf_1")
        xf_23 = tile([P, 2, T], F32, "xf_23")
        xo_01 = tile([P, 2, Z], F32, "xo_01")
        xo_2 = tile([P, Z], F32, "xo_2")
        fk_sb = tile([P, PACK], F32, "fk_sb")
        fl_sb = tile([P, PACK], F32, "fl_sb")
        w2_raw_scale = tile([P, R], U8, "w2_raw_scale")
        q_sb = tile([P, PACK, LEAD + J], F32, "q_sb")

        def load_words(dst, words):
            nc.sync.dma_start(out=dst[:].bitcast(I32), in_=words[0].rearrange("p n t -> p (n t)").bitcast(I32))

        def load_scales(dst, scales):
            nc.gpsimd.memset(dst[:].bitcast(U32), 0)
            for quad in range(QUADS):
                nc.sync.dma_start(
                    out=dst[32 * quad : 32 * quad + 4, :].bitcast(I32),
                    in_=scales[0, 4 * quad : 4 * quad + 4, :].bitcast(I32),
                )

        nc.gpsimd.memset(q_sb[:, :, 0:LEAD], 0.0)

        xf_rows = xf.rearrange("(p t) c -> p t c", t=PACK)
        xo_rows = xo.rearrange("(p t) c -> p t c", t=PACK)
        so_rows = so.rearrange("(p t) j -> p t j", t=PACK)
        nc.sync.dma_start(out=gate_first[:], in_=so_rows[:, 0, :])
        nc.sync.dma_start(list1[:], offs)
        nc.sync.dma_start(list2[:], offs2)
        nc.sync.dma_start(out=xf_0[:], in_=xf_rows[:, 0, :])
        nc.sync.dma_start(out=xf_1[:], in_=xf_rows[:, 1, :])
        nc.sync.dma_start(out=xf_23[:], in_=xf_rows[:, 2:4, :])
        nc.sync.dma_start(out=fk_sb[:], in_=fk.rearrange("(p t) o -> p (t o)", t=PACK))
        nc.sync.dma_start(out=gate_rest[:], in_=so_rows[:, 1:PACK, :])
        nc.sync.dma_start(list3[:], offs3)
        nc.sync.dma_start(out=fl_sb[:], in_=fl.rearrange("(p t) o -> p (t o)", t=PACK))
        nc.sync.dma_start(out=xo_01[:], in_=xo_rows[:, 0:2, :])
        nc.sync.dma_start(out=xo_2[:], in_=xo_rows[:, 2, :])
        load_scales(w2_raw_scale, w2_scales)

        def gather(on_vector, dst, window, offsets):
            if on_vector:
                nc.vector.tensor_copy(dst, window.indirect(offsets))
            else:
                nc.scalar.activation(dst, window.indirect(offsets), ACT.Copy)

        def weave(ap):
            return ap.rearrange("p (c i) t -> p c t i", i=4)

        def planes(ap):
            return ap.rearrange("p t (c i) -> p c t i", i=4)

        gate = tile([P, PACK, J], F32, "gate")
        nc.scalar.activation(gate[:, 0, :], gate_first[:], ACT.Sigmoid)

        xo_last = tile([P, Z], F32, "xo_last", tag="gate_first")
        nc.sync.dma_start(out=xo_last[:], in_=xo_rows[:, PACK - 1, :])

        pick1 = tile([P, PACK, J], F32, "pick1")
        pick2 = tile([P, PACK, J], F32, "pick2")
        larger = tile([P, PACK, J], F32, "larger")
        for t in range(PACK):
            window = (xf_0[:], xf_1[:], xf_23[:, 0, :], xf_23[:, 1, :])[t]
            gather(t < 3, pick1[:, t, :], window, list1[:])
            gather(False, pick2[:, t, :], window, list2[:])
            nc.vector.tensor_tensor(larger[:, t, :], pick1[:, t, :], pick2[:, t, :], ALU.max)
        nc.scalar.activation(gate[:, 1:PACK, :], gate_rest[:], ACT.Sigmoid)
        w2_raw = tile([P, R], U32, "w2_raw", tag="xf_0")
        load_words(w2_raw, w2_words)
        w_raw = tile([P, R], U32, "w_raw", tag="xf_1")
        load_words(w_raw, w_words)
        w_raw_scale = tile([P, R], U8, "w_raw_scale", tag="xf_23")
        load_scales(w_raw_scale, w_scales)
        wb_codes = tile([P, N], U32, "wb_codes", tag="gate_rest")
        load_words(wb_codes, wb_words)
        rs_sb = tile([P, HALVES, N], F32, "rs_sb", tag="pick1")
        nc.sync.dma_start(out=rs_sb[:], in_=rs.rearrange("(h p) n -> p h n", p=P))
        u_bf = tile([P, J, PACK], BF16, "u_bf")
        nc.vector.tensor_tensor(
            weave(u_bf[:]),
            planes(larger[:]),
            fk_sb[:].unsqueeze(1).unsqueeze(3).to_broadcast([P, J // 4, PACK, 4]),
            ALU.mult,
        )
        wb_scale = tile([P, N], U8, "wb_scale", tag="pick2")
        load_scales(wb_scale, wb_scales)
        u_codes = tile([P, J], U32, "u_codes")
        u_scale = tile([P, J], U8, "u_scale")
        nc.vector.quantize_mx(out=u_codes[:].bitcast(E5M2), scales=u_scale[:], in_=u_bf[:].rearrange("p j t -> p (j t)"))

        def deal_scales(dst, src):
            nc.vector.tensor_copy(
                dst[:].rearrange("p (t c i) -> p c t i", t=PACK, i=16),
                src[:].rearrange("p (c i t) -> p c t i", t=PACK, i=16),
            )

        factor = tile([P, PACK, J], F32, "factor", tag="larger")
        for t in range(PACK):
            nc.vector.tensor_scalar(factor[:, t, :], gate[:, t, :], fl_sb[:, t : t + 1], None, ALU.mult)
        w2_scale = tile([P, R], U8, "w2_scale", tag="u_bf")
        deal_scales(w2_scale, w2_raw_scale)

        pick3 = tile([P, PACK, J], F32, "pick3")
        for t in range(PACK - 1):
            gather(False, pick3[:, t, :], (xo_01[:, 0, :], xo_01[:, 1, :], xo_2[:])[t], list3[:])
        last = PACK - 1
        for h in range(HALVES):
            cols = slice(h * HALF, (h + 1) * HALF)
            gather(h == 0, pick3[:, last, cols], xo_last[:], list3[:, h * 8 : (h + 1) * 8])

        w2_codes = tile([P, R], U32, "w2_codes", tag="gate_first")

        def deal_words(dst, src):
            nc.scalar.copy(
                dst[:].rearrange("p (t c i) -> p c t i", t=PACK, i=4),
                src[:].rearrange("p (c i t) -> p c t i", t=PACK, i=4),
            )

        deal_words(w2_codes, w2_raw)
        u2_codes = [tile([P, HALF], U32, "u2_codes%d" % h) for h in range(HALVES)]
        u2_scale = [tile([P, HALF], U8, "u2_scale%d" % h) for h in range(HALVES)]
        w_codes = tile([P, R], U32, "w_codes", tag="xf_0")
        deal_words(w_codes, w_raw)

        q_ps = [[psum.tile([P, 2, HALF], F32, name="q_ps%d%d" % (h, u)) for u in range(2)] for h in range(HALVES)]
        a_ps = [psum.tile([P, PACK, HALF], F32, name="a_ps%d" % h) for h in range(HALVES)]
        p_ps = [psum.tile([P, N], F32, name="p_ps%d" % h) for h in range(HALVES)]

        def first_stage(acc, t, codes, scale, rhs, rhs_scale):
            cols = slice(t * P, (t + 1) * P)
            nc.tensor.matmul_mx(
                out=acc,
                lhsT=codes[:, cols].bitcast(E5M2),
                lhsT_scale=scale[:, cols],
                rhs=rhs,
                rhs_scale=rhs_scale,
                start=True,
                stop=True,
            )

        u2_bf = [tile([P, HALF, PACK], BF16, "u2_bf%d" % h, tag=("u2_bf0", "u2_bf1")[h]) for h in range(HALVES)]
        for h in range(HALVES):
            cols = slice(h * HALF, (h + 1) * HALF)
            nc.vector.tensor_tensor(weave(u2_bf[h][:]), planes(pick3[:, :, cols]), planes(factor[:, :, cols]), ALU.mult)
            nc.vector.quantize_mx(
                out=u2_codes[h][:].bitcast(E4M3), scales=u2_scale[h][:], in_=u2_bf[h][:].rearrange("p j t -> p (j t)")
            )
            for t in range(PACK):
                first_stage(q_ps[h][t // 2][:, t % 2, :], t, w2_codes, w2_scale, u2_codes[h][:].bitcast(E4M3), u2_scale[h][:])
        w_scale = tile([P, R], U8, "w_scale", tag="u2_bf1")
        deal_scales(w_scale, w_raw_scale)
        for h in range(HALVES):
            cols = slice(h * HALF, (h + 1) * HALF)
            for t in range(PACK):
                first_stage(a_ps[h][:, t, :], t, w_codes, w_scale, u_codes[:, cols].bitcast(E5M2), u_scale[:, cols])

        steps = tile([P, PACK, J], F32, "steps", tag="xf_23")
        for h in range(HALVES):
            for u in range(2):
                nc.scalar.copy(q_sb[:, 2 * u : 2 * u + 2, LEAD + h * HALF : LEAD + (h + 1) * HALF], q_ps[h][u][:])

        rs_scaled = tile([P, HALVES, N], F32, "rs_scaled", tag="u2_codes1")
        nc.scalar.activation(rs_scaled[:], rs_sb[:], ACT.Copy, scale=-0.3)

        p_twin = []
        for h in range(HALVES):
            cols = slice(h * HALF, (h + 1) * HALF)
            for u in range(2):
                nc.vector.scalar_tensor_tensor(
                    steps[:, 2 * u : 2 * u + 2, cols],
                    q_sb[:, 2 * u : 2 * u + 2, LEAD - 1 + h * HALF : LEAD - 1 + (h + 1) * HALF],
                    -0.6,
                    q_ps[h][u][:],
                    ALU.mult,
                    ALU.add,
                )
            hid_bf = tile([P, HALF, PACK], BF16, "hid_bf%d" % h)
            hid_codes = tile([P, HALF], U32, "hid_codes%d" % h)
            hid_scale = tile([P, HALF], U8, "hid_scale%d" % h)
            nc.vector.tensor_tensor(weave(hid_bf[:]), planes(steps[:, :, cols]), planes(a_ps[h][:]), ALU.max)
            nc.vector.quantize_mx(
                out=hid_codes[:].bitcast(E5M2), scales=hid_scale[:], in_=hid_bf[:].rearrange("p j t -> p (j t)")
            )
            twin = psum.tile([P, N], F32, name="p_twin%d" % h, tag="q_ps0%d" % h)
            p_twin.append(twin)
            for acc in (twin, p_ps[h]):
                nc.tensor.matmul_mx(
                    out=acc[:],
                    lhsT=hid_codes[:].bitcast(E5M2),
                    lhsT_scale=hid_scale[:],
                    rhs=wb_codes[:].bitcast(E4M3),
                    rhs_scale=wb_scale[:],
                    start=True,
                    stop=True,
                )

        for h in range(HALVES):
            magnitude = tile([P, N], F32, "magnitude%d" % h)
            mean = tile([P, 1], F32, "mean%d" % h)
            shifted = tile([P, N], F32, "shifted%d" % h)
            result = tile([P, N], F32, "result%d" % h)
            nc.scalar.activation(magnitude[:], p_twin[h][:], ACT.Abs, scale=1.0 / N, accum_out=mean[:])
            nc.vector.tensor_tensor(shifted[:], p_ps[h][:], rs_scaled[:, h, :], ALU.add)
            nc.vector.scalar_tensor_tensor(result[:], shifted[:], mean[:], rs_scaled[:, h, :], ALU.subtract, ALU.max)
            nc.sync.dma_start(out=out[h * HALF : (h + 1) * HALF, :], in_=result[:])
